import numpy as np
import ml_dtypes


def mxq(x, axis, fmt="e4m3"):
    dtype, down = {"e4m3": (ml_dtypes.float8_e4m3fn, 7), "e5m2": (ml_dtypes.float8_e5m2, 14)}[fmt]
    v = np.moveaxis(np.asarray(x, np.float32).astype(ml_dtypes.bfloat16).astype(np.float64), axis, -1)
    blocks = v.reshape(v.shape[:-1] + (-1, 32))
    amax = np.abs(blocks).max(-1, keepdims=True)
    byte = np.maximum(np.where(amax > 0, np.frexp(amax)[1] - 1 + 127, 0) - down, 1)
    scale = np.exp2(byte - 127.0)
    codes = (blocks / scale).astype(np.float32).astype(dtype).astype(np.float64)
    return np.moveaxis((codes * scale).reshape(v.shape), -1, axis)


WIDE = False


def mx_kscale(k):
    if not WIDE:
        return np.ones(k)
    levels = np.array([10, -10, 5, -5, 0])
    if k % 512:
        return np.exp2(np.random.permutation(np.resize(levels, k // 32))).repeat(32)
    a = np.empty((k // 512, 16))
    for p in range(k // 512):
        a[p, :8] = np.random.permutation(np.resize(levels, 8))
        for g in range(8):
            far = levels[np.abs(levels - a[p, g]) >= 10]
            a[p, g + 8] = far[np.random.randint(len(far))]
    return np.exp2(a.ravel()).repeat(32)


def f64(x):
    return np.asarray(x).astype(np.float64)


def striped(idx):
    return np.tile(idx.reshape(-1, 16).T, (8, 1)).astype(np.uint16)


def unstriped(offs):
    return offs[:16].T.reshape(-1).astype(np.int64)


E2M1 = np.array([0.0, 0.5, 1.0, 1.5, 2.0, 3.0, 4.0, 6.0, -0.0, -0.5, -1.0, -1.5, -2.0, -3.0, -4.0, -6.0])


def pack_weight(w, fmt):
    k, n = w.shape
    w = f64(np.asarray(w, np.float32).astype(ml_dtypes.bfloat16)).reshape(k // 32, 32, n)
    amax = np.abs(w).max(1)
    if fmt == "e4m3":
        byte = np.frexp(amax)[1] - 1 + 127 - 7
    else:
        mant, ex = np.frexp(amax / 6.0)
        byte = np.where(mant > 0.5, ex, ex - 1) + 127
    byte = np.clip(np.where(amax > 0, byte, 1), 1, 254)
    scaled = (w * np.exp2(127.0 - byte)[:, None, :]).reshape(k, n).astype(np.float32)
    by_word = np.ascontiguousarray(scaled.reshape(k // 512, 128, 4, n).transpose(0, 1, 3, 2))
    if fmt == "e4m3":
        words = by_word.astype(ml_dtypes.float8_e4m3fn).view(np.uint8)
    else:
        c = by_word.astype(ml_dtypes.float4_e2m1fn).view(np.uint8) & 0xF
        words = (c[..., 0::2] | (c[..., 1::2] << 4)).reshape(k // 512, 128, 2 * n)
    return np.ascontiguousarray(words), np.ascontiguousarray(byte.astype(np.uint8).reshape(k // 512, 16, n))


def unpack_weight(words, scales, fmt):
    g, _, n = scales.shape
    words = np.ascontiguousarray(words).reshape(g, 128, n, -1)
    if fmt == "e4m3":
        vals = words.view(ml_dtypes.float8_e4m3fn).astype(np.float64)
    else:
        nib = np.empty((g, 128, n, 4), np.uint8)
        nib[..., 0::2] = words & 0xF
        nib[..., 1::2] = words >> 4
        vals = E2M1[nib]
    vals = vals * np.repeat(np.exp2(scales.astype(np.float64) - 127.0), 8, axis=1)[..., None]
    return vals.transpose(0, 1, 3, 2).reshape(g * 512, n)


def gelu(v):
    return 0.5 * v * (1.0 + np.tanh(np.sqrt(2.0 / np.pi) * (v + 0.044715 * v**3)))


K, H, T, S, P = 1024, 1024, 4096, 1024, 512


def setup_inputs():
    n = np.random.standard_normal
    s = mx_kscale(K)[:, None]
    u = mx_kscale(H)[:, None]
    tab_words, tab_scales = pack_weight(n((K, T)) * s, "e4m3")
    w4_words, w4_scales = pack_weight(1.2 * n((K, H)) / np.sqrt(K) / s, "e2m1")
    return {
        "tab_words": tab_words,
        "tab_scales": tab_scales,
        "offs": striped(np.random.permutation(T)[:S]),
        "pos1": striped(np.random.permutation(S)[:P]),
        "pos2": striped(np.random.permutation(S)[:P]),
        "w1": (n((K, H)) / np.sqrt(K) / s * u.T).astype(np.float32),
        "w4_words": w4_words,
        "w4_scales": w4_scales,
        "gain": (0.6 * np.exp(0.5 * n(H))).astype(np.float32),
        "chan": (np.exp(0.3 * n(H)) / np.sqrt(H) / u[:, 0] ** 2).astype(np.float32),
        "base": (0.8 * n((P, P))).astype(np.float32),
        "fin": np.exp(0.4 * n(P)).astype(np.float32),
    }


def reference(tab_words, tab_scales, offs, pos1, pos2, w1, w4_words, w4_scales, gain, chan, base, fin):
    v = unpack_weight(tab_words, tab_scales, "e4m3")[:, unstriped(offs)]
    w4 = unpack_weight(w4_words, w4_scales, "e2m1")
    drive = mxq(f64(w1), 0, "e4m3").T @ v
    turn = w4.T @ v
    h = drive * (f64(gain)[:, None] + np.tanh(turn))
    x1 = h[:, unstriped(pos1)]
    x2 = np.abs(h[:, unstriped(pos2)]) * f64(chan)[:, None]
    e = mxq(x1, 0, "e4m3").T @ mxq(x2, 0, "e4m3")
    return (e + f64(base)) * f64(fin)[None, :]

@@ -1,0 +1,299 @@
+from contextlib import ExitStack
+
+import concourse.mybir as mybir
+from concourse.masks import make_identity
+
+K, H, T, S, PICK = 1024, 1024, 4096, 1024, 512
+FLOPS = 2 * (2 * K * H * S + H * PICK * PICK)
+
+F32 = mybir.dt.float32
+BF16 = mybir.dt.bfloat16
+I32 = mybir.dt.int32
+U32 = mybir.dt.uint32
+U16 = mybir.dt.uint16
+U8 = mybir.dt.uint8
+FP8X4 = mybir.dt.float8_e4m3fn_x4
+FP4X4 = mybir.dt.float4_e2m1fn_x4
+ALU = mybir.AluOpType
+ACT = mybir.ActivationFunctionType
+
+P = 128
+PASS = 512
+BANK = 512
+PACK = 4
+
+
+def tile_list_leadout_handover_scores_kernel(
+    tc, tab_words, tab_scales, offs, pos1, pos2, w1, w4_words, w4_scales, gain, chan, base, fin, out
+):
+    nc = tc.nc
+    with ExitStack() as ctx:
+        lists = ctx.enter_context(tc.tile_pool(name="lists", bufs=1))
+        keep = ctx.enter_context(tc.tile_pool(name="keep", bufs=1))
+        ring = ctx.enter_context(tc.tile_pool(name="ring", bufs=2))
+        psum = ctx.enter_context(tc.psum_pool(name="psum", bufs=1))
+
+        offs_sb = lists.tile([P, S // 16], U16, name="offs_sb")
+        pos1_sb = lists.tile([P, PICK // 16], U16, name="pos1_sb")
+        pos2_sb = lists.tile([P, PICK // 16], U16, name="pos2_sb")
+
+        def held(shape, dtype, name, tag=None):
+            return keep.tile(shape, dtype, name=name, tag=tag or name, align_bytes=64)
+
+        nc.sync.dma_start(offs_sb[:], offs)
+        scale_rows = held([P, T], U8, "scale_rows")
+        nc.sync.dma_start(
+            scale_rows[0:32, :].bitcast(I32), tab_scales.rearrange("a q t -> (a q) t").bitcast(I32)
+        )
+        w4_rows = held([32, H], U8, "w4_rows")
+        nc.sync.dma_start(w4_rows[:].bitcast(I32), w4_scales.rearrange("a q c -> (a q) c").bitcast(I32))
+        nc.sync.dma_start(pos1_sb[:], pos1)
+        nc.sync.dma_start(pos2_sb[:], pos2)
+
+        def load_table(a, tag):
+            words = held([P, T], U32, "tab_words%d" % a, tag)
+            nc.sync.dma_start(words[:].bitcast(I32), tab_words[a].rearrange("p t i -> p (t i)").bitcast(I32))
+            return words
+
+        def load_w1(a, b, tag):
+            raw = held([P, PACK, PASS], F32, "w1_raw%d%d" % (a, b), tag)
+            rows = w1[PASS * a : PASS * (a + 1), PASS * b : PASS * (b + 1)]
+            nc.sync.dma_start(raw[:], rows.rearrange("(p j) c -> p j c", j=PACK))
+            return raw
+
+        table0 = load_table(0, "stream_a")
+        w4_raw = held([P, 2, 2 * H], U8, "w4_raw", "stream_c")
+        nc.sync.dma_start(w4_raw[:].bitcast(I32), w4_words.rearrange("a p c -> p a c").bitcast(I32))
+        table1 = load_table(1, "stream_b")
+
+        rows_gc = held([P, 2 * P], F32, "rows_gc")
+        nc.gpsimd.memset(rows_gc[:], 0.0)
+        nc.vector.memset(scale_rows[32:64, :].bitcast(I32), 0)
+        nc.vector.memset(scale_rows[64:128, :].bitcast(I32), 0)
+        planes = held([P, 2, S + H], U8, "planes")
+        nc.vector.memset(planes[:].bitcast(I32), 0)
+        v_scales = [planes[:, a, 0:S] for a in range(2)]
+        w4_sc = [planes[:, a, S : S + H] for a in range(2)]
+        for v, vec in enumerate((gain, chan)):
+            nc.gpsimd.dma_start(
+                rows_gc[4 * v : 4 * v + 4, :].rearrange("t (g q) -> t g q", q=8),
+                vec.rearrange("(g t q) -> t g q", t=4, q=8),
+            )
+        ident = held([P, P], F32, "ident")
+        make_identity(nc, ident[:])
+
+        picked_rows = held([P, S], U8, "picked_rows")
+        staged = held([32, 2, S + H], U8, "staged")
+        nc.vector.tensor_copy(picked_rows[:], scale_rows[:].indirect(offs_sb[:]))
+        nc.vector.tensor_copy(
+            staged[:, 0, S : S + H].bitcast(I32).rearrange("p (b t g w) -> p b t g w", b=2, t=4, w=2),
+            w4_rows[:].bitcast(I32).rearrange("p (b g t w) -> p b t g w", b=2, t=4, w=2),
+        )
+        nc.vector.tensor_copy(staged[:, 0, 0:S].bitcast(I32), picked_rows[0:32, :].bitcast(I32))
+        nc.scalar.dma_start(staged[0:16, 1, :].bitcast(I32), staged[16:32, 0, :].bitcast(I32))
+        for q in range(4):
+            nc.scalar.dma_start(
+                planes[32 * q : 32 * q + 4, :, :].bitcast(I32), staged[4 * q : 4 * q + 4, :, :].bitcast(I32)
+            )
+
+        gc_bank = psum.tile([P, 2, P], F32, name="gc_bank", tag="bank30")
+        for b in range(2):
+            nc.tensor.transpose(gc_bank[:, b, :], rows_gc[:, P * b : P * (b + 1)], ident[:])
+        gc = held([P, 16], F32, "gc")
+        nc.scalar.copy(
+            gc[:].rearrange("p (v b t) -> p v b t", v=2, b=2),
+            gc_bank[:, :, 0:8].rearrange("p b (v t) -> p v b t", v=2),
+        )
+        step01 = held([P, 8], F32, "step01")
+        sign = held([P, 8], F32, "sign")
+        sgain = held([P, 8], F32, "sgain")
+
+        v_words = {}
+
+        def gather_words(a, half, table):
+            v_words[a, half] = held([P, BANK], U32, "v_words%d%d" % (a, half))
+            cols = slice(half * BANK // 16, (half + 1) * BANK // 16)
+            nc.vector.tensor_copy(v_words[a, half][:], table[:].indirect(offs_sb[:, cols]))
+
+        w1_bf, w1_codes, w1_scales = {}, {}, {}
+
+        def round_w1(a, b, t, copy=nc.scalar.copy, into=None):
+            if into is None:
+                into = ring.tile([P, P, PACK], BF16, name="w1_bf", tag="w1_bf", bufs=8, align_bytes=64)
+            w1_bf[a, b, t] = into
+            src = w1_raw[a, b][:].rearrange("p j (g t h i) -> p t g h j i", t=4, h=2, i=4)[:, t]
+            dst = w1_bf[a, b, t][:].rearrange("p (g h i) j -> p g h j i", h=2, i=4)
+            copy(dst, src)
+
+        def quant_w1(a, b, t):
+            w1_codes[a, b, t] = held([P, P], U32, "w1_codes%d%d%d" % (a, b, t))
+            w1_scales[a, b, t] = held([P, P], U8, "w1_scales%d%d%d" % (a, b, t))
+            nc.vector.quantize_mx(
+                out=w1_codes[a, b, t][:].bitcast(FP8X4),
+                scales=w1_scales[a, b, t][:],
+                in_=w1_bf[a, b, t][:].rearrange("p c j -> p (c j)"),
+            )
+
+        gather_words(0, 0, table0)
+        gather_words(0, 1, table0)
+        w1_raw = {(0, 0): load_w1(0, 0, "stream_a")}
+
+        nc.vector.tensor_scalar(step01[:], gc[:, 8:16], 0.0, 2.0, ALU.is_ge, ALU.mult)
+        w4_codes = held([P, 2, 2 * H], U8, "w4_codes")
+        nc.vector.tensor_copy(
+            w4_codes[:].bitcast(I32).rearrange("p a (b t g w) -> p (a b) t g w", b=2, t=4, w=4),
+            w4_raw[:].bitcast(I32).rearrange("p a (b g t w) -> p (a b) t g w", b=2, t=4, w=4),
+        )
+        w1_raw[1, 0] = load_w1(1, 0, "stream_c")
+        nc.vector.tensor_scalar(sign[:], step01[:], -1.0, None, ALU.add)
+        gather_words(1, 0, table1)
+        nc.vector.tensor_tensor(sgain[:], gc[:, 0:8], sign[:], ALU.mult)
+        gather_words(1, 1, table1)
+        first_bf = held([P, 4, P, PACK], BF16, "first_bf", "stream_b")
+        for t in range(4):
+            round_w1(0, 0, t, nc.vector.tensor_copy, first_bf[:, t])
+        w1_raw[1, 1] = load_w1(1, 1, "stream_a")
+        for t in range(4):
+            quant_w1(0, 0, t)
+        w1_raw[0, 1] = load_w1(0, 1, "stream_b")
+
+        tanh_sb, drive_bank, h = {}, {}, {}
+
+        def turn(s):
+            for half in range(2):
+                bank = psum.tile([P, BANK], F32, name="turn_bank", tag="bank%d%d" % (s % 4, half))
+                cols = slice(half * BANK, (half + 1) * BANK)
+                for a in range(2):
+                    nc.tensor.matmul_mx(
+                        out=bank[:],
+                        lhsT=w4_codes[:, a, 2 * P * s : 2 * P * (s + 1)].bitcast(FP4X4),
+                        lhsT_scale=w4_sc[a][:, P * s : P * (s + 1)],
+                        rhs=v_words[a, half][:].bitcast(FP8X4),
+                        rhs_scale=v_scales[a][:, cols],
+                        start=(a == 0),
+                        stop=(a == 1),
+                    )
+                tanh_sb[s, half] = ring.tile([P, BANK], F32, name="tanh_sb", tag="tanh_sb", bufs=6)
+                nc.scalar.activation(tanh_sb[s, half][:], bank[:], ACT.Tanh, scale=sign[:, s : s + 1])
+
+        def drive(s):
+            b, t = divmod(s, 4)
+            for half in range(2):
+                drive_bank[s, half] = psum.tile([P, BANK], F32, name="drive_bank", tag="bank%d%d" % ((s + 2) % 4, half))
+                cols = slice(half * BANK, (half + 1) * BANK)
+                for a in range(2):
+                    nc.tensor.matmul_mx(
+                        out=drive_bank[s, half][:],
+                        lhsT=w1_codes[a, b, t][:].bitcast(FP8X4),
+                        lhsT_scale=w1_scales[a, b, t][:],
+                        rhs=v_words[a, half][:].bitcast(FP8X4),
+                        rhs_scale=v_scales[a][:, cols],
+                        start=(a == 0),
+                        stop=(a == 1),
+                    )
+
+        def combine(s):
+            h[s] = ring.tile([P, S], F32, name="h", tag="h", bufs=3)
+            for half in range(2):
+                nc.vector.scalar_tensor_tensor(
+                    h[s][:, half * BANK : (half + 1) * BANK],
+                    tanh_sb[s, half][:],
+                    sgain[:, s : s + 1],
+                    drive_bank[s, half][:],
+                    ALU.add,
+                    ALU.mult,
+                )
+
+        x_planes = {}
+        for b in range(2):
+            for side in range(2):
+                x_planes[side, b] = held([P, PACK, PICK], BF16, "x_planes%d%d" % (side, b))
+
+        def pick(s):
+            b, t = divmod(s, 4)
+            picked2 = ring.tile([P, PICK], F32, name="picked2", tag="picked2", bufs=3)
+            nc.vector.tensor_copy(picked2[:], h[s][:].indirect(pos2_sb[:]))
+            nc.vector.tensor_copy(x_planes[0, b][:, t, :], h[s][:].indirect(pos1_sb[:]))
+            nc.scalar.activation(x_planes[1, b][:, t, :], picked2[:], ACT.Abs, scale=gc[:, 8 + s : 9 + s])
+
+        x_bf, x_codes, x_scales = {}, {}, {}
+
+        def weave(side, b, copy=nc.scalar.copy):
+            x_bf[side, b] = held([P, PICK, PACK], BF16, "x_bf%d%d" % (side, b))
+            copy(
+                x_bf[side, b][:].rearrange("p (c i) t -> p c t i", i=4),
+                x_planes[side, b][:].rearrange("p t (c i) -> p c t i", i=4),
+            )
+
+        def quant_x(side, b):
+            x_codes[side, b] = held([P, PICK], U32, "x_codes%d%d" % (side, b))
+            x_scales[side, b] = held([P, PICK], U8, "x_scales%d%d" % (side, b))
+            nc.vector.quantize_mx(
+                out=x_codes[side, b][:].bitcast(FP8X4),
+                scales=x_scales[side, b][:],
+                in_=x_bf[side, b][:].rearrange("p c t -> p (c t)"),
+            )
+
+        turn(0)
+        turn(1)
+        round_w1(1, 0, 0, nc.vector.tensor_copy)
+        round_w1(1, 0, 1, nc.vector.tensor_copy)
+        quant_w1(1, 0, 0)
+        quant_w1(1, 0, 1)
+        drive(0)
+        drive(1)
+        combine(0)
+        for s in range(1, 8):
+            nxt = s + 1
+            if nxt < 8:
+                b, t = divmod(nxt, 4)
+                turn(nxt)
+                if b == 1:
+                    round_w1(0, 1, t)
+                    quant_w1(0, 1, t)
+                round_w1(1, b, t)
+                quant_w1(1, b, t)
+                drive(nxt)
+            combine(s)
+            pick(s - 1)
+            if s == 4:
+                weave(1, 0)
+                weave(0, 0)
+            if s == 6:
+                quant_x(1, 0)
+                quant_x(0, 0)
+        base_sb = held([P, 4, PICK], F32, "base_sb", "stream_c")
+        nc.sync.dma_start(base_sb[:], base.rearrange("(m p) j -> p m j", p=P))
+        fin_sb = held([P, PICK], F32, "fin_sb", "stream_b")
+        nc.sync.dma_start(fin_sb[:], fin.partition_broadcast(P))
+        pick(7)
+        weave(1, 1)
+        weave(0, 1, nc.vector.tensor_copy)
+        quant_x(0, 1)
+        quant_x(1, 1)
+
+        sums = []
+        for m in range(4):
+            bank = psum.tile([P, PICK], F32, name="score_bank", tag="bank%d%d" % (2 + m // 2, m % 2))
+            for b in range(2):
+                nc.tensor.matmul_mx(
+                    out=bank[:],
+                    lhsT=x_codes[0, b][:, P * m : P * (m + 1)].bitcast(FP8X4),
+                    lhsT_scale=x_scales[0, b][:, P * m : P * (m + 1)],
+                    rhs=x_codes[1, b][:].bitcast(FP8X4),
+                    rhs_scale=x_scales[1, b][:],
+                    start=(b == 0),
+                    stop=(b == 1),
+                )
+            total = held([P, PICK], F32, "total%d" % m)
+            nc.vector.tensor_tensor(total[:], bank[:], base_sb[:, m, :], ALU.add)
+            sums.append(total)
+            if m > 0:
+                finish(nc, held, sums[m - 1], fin_sb, out, m - 1)
+        finish(nc, held, sums[3], fin_sb, out, 3)
+
+
+def finish(nc, held, total, fin_sb, out, m):
+    result = held([P, PICK], F32, "result%d" % m)
+    nc.vector.tensor_tensor(result[:], total[:], fin_sb[:], ALU.mult)
+    nc.sync.dma_start(out[P * m : P * (m + 1), :], result[:])

@@ -47,38 +47,39 @@ def tile_list_leadout_handover_scores_kernel(
         )
         w4_rows = held([32, H], U8, "w4_rows")
         nc.sync.dma_start(w4_rows[:].bitcast(I32), w4_scales.rearrange("a q c -> (a q) c").bitcast(I32))
-        nc.sync.dma_start(pos1_sb[:], pos1)
-        nc.sync.dma_start(pos2_sb[:], pos2)
 
         def load_table(a, tag):
             words = held([P, T], U32, "tab_words%d" % a, tag)
             nc.sync.dma_start(words[:].bitcast(I32), tab_words[a].rearrange("p t i -> p (t i)").bitcast(I32))
             return words
 
-        def load_w1(a, b, tag):
-            raw = held([P, PACK, PASS], F32, "w1_raw%d%d" % (a, b), tag)
+        def load_w1(a, b, raw):
             rows = w1[PASS * a : PASS * (a + 1), PASS * b : PASS * (b + 1)]
-            nc.sync.dma_start(raw[:], rows.rearrange("(p j) c -> p j c", j=PACK))
-            return raw
+            nc.sync.dma_start(raw, rows.rearrange("(p j) c -> p j c", j=PACK))
 
         table0 = load_table(0, "stream_a")
-        w4_raw = held([P, 2, 2 * H], U8, "w4_raw", "stream_c")
+        w4_raw = held([P, 2, 2 * H], U8, "w4_raw")
         nc.sync.dma_start(w4_raw[:].bitcast(I32), w4_words.rearrange("a p c -> p a c").bitcast(I32))
-        table1 = load_table(1, "stream_b")
+        nc.sync.dma_start(pos1_sb[:], pos1)
+        nc.sync.dma_start(pos2_sb[:], pos2)
 
         rows_gc = held([P, 2 * P], F32, "rows_gc")
         nc.gpsimd.memset(rows_gc[:], 0.0)
         nc.vector.memset(scale_rows[32:64, :].bitcast(I32), 0)
         nc.vector.memset(scale_rows[64:128, :].bitcast(I32), 0)
         planes = held([P, 2, S + H], U8, "planes")
-        nc.vector.memset(planes[:].bitcast(I32), 0)
+        nc.gpsimd.memset(planes[:].bitcast(I32), 0)
         v_scales = [planes[:, a, 0:S] for a in range(2)]
         w4_sc = [planes[:, a, S : S + H] for a in range(2)]
         for v, vec in enumerate((gain, chan)):
-            nc.gpsimd.dma_start(
+            nc.sync.dma_start(
                 rows_gc[4 * v : 4 * v + 4, :].rearrange("t (g q) -> t g q", q=8),
                 vec.rearrange("(g t q) -> t g q", t=4, q=8),
             )
+        w1_raw = {(a, 0): held([P, PACK, PASS], F32, "w1_first%d" % a) for a in range(2)}
+        for a in range(2):
+            load_w1(a, 0, w1_raw[a, 0][:])
+        table1 = load_table(1, "stream_b")
         ident = held([P, P], F32, "ident")
         make_identity(nc, ident[:])
 
@@ -117,13 +118,11 @@ def tile_list_leadout_handover_scores_kernel(
 
         w1_bf, w1_codes, w1_scales = {}, {}, {}
 
-        def round_w1(a, b, t, copy=nc.scalar.copy, into=None):
-            if into is None:
-                into = ring.tile([P, P, PACK], BF16, name="w1_bf", tag="w1_bf", bufs=8, align_bytes=64)
-            w1_bf[a, b, t] = into
-            src = w1_raw[a, b][:].rearrange("p j (g t h i) -> p t g h j i", t=4, h=2, i=4)[:, t]
-            dst = w1_bf[a, b, t][:].rearrange("p (g h i) j -> p g h j i", h=2, i=4)
-            copy(dst, src)
+        def round_w1(a, b, t):
+            w1_bf[a, b, t] = ring.tile([P, P, PACK], BF16, name="w1_bf", tag="w1_bf", bufs=4, align_bytes=64)
+            src = w1_raw[a, b][:].rearrange("p j (g t q) -> p t g q j", t=4, q=8)[:, t]
+            dst = w1_bf[a, b, t][:].rearrange("p (g q) j -> p g q j", q=8)
+            (nc.vector.tensor_copy, nc.scalar.copy)[b](dst, src)
 
         def quant_w1(a, b, t):
             w1_codes[a, b, t] = held([P, P], U32, "w1_codes%d%d%d" % (a, b, t))
@@ -136,73 +135,64 @@ def tile_list_leadout_handover_scores_kernel(
 
         gather_words(0, 0, table0)
         gather_words(0, 1, table0)
-        w1_raw = {(0, 0): load_w1(0, 0, "stream_a")}
-
-        nc.vector.tensor_scalar(step01[:], gc[:, 8:16], 0.0, 2.0, ALU.is_ge, ALU.mult)
         w4_codes = held([P, 2, 2 * H], U8, "w4_codes")
         nc.vector.tensor_copy(
             w4_codes[:].bitcast(I32).rearrange("p a (b t g w) -> p (a b) t g w", b=2, t=4, w=4),
             w4_raw[:].bitcast(I32).rearrange("p a (b g t w) -> p (a b) t g w", b=2, t=4, w=4),
         )
-        w1_raw[1, 0] = load_w1(1, 0, "stream_c")
+        nc.vector.tensor_scalar(step01[:], gc[:, 8:16], 0.0, 2.0, ALU.is_ge, ALU.mult)
         nc.vector.tensor_scalar(sign[:], step01[:], -1.0, None, ALU.add)
-        gather_words(1, 0, table1)
         nc.vector.tensor_tensor(sgain[:], gc[:, 0:8], sign[:], ALU.mult)
+        for a in range(2):
+            for t in range(4):
+                round_w1(a, 0, t)
+            for t in range(4):
+                quant_w1(a, 0, t)
+        gather_words(1, 0, table1)
         gather_words(1, 1, table1)
-        first_bf = held([P, 4, P, PACK], BF16, "first_bf", "stream_b")
-        for t in range(4):
-            round_w1(0, 0, t, nc.vector.tensor_copy, first_bf[:, t])
-        w1_raw[1, 1] = load_w1(1, 1, "stream_a")
-        for t in range(4):
-            quant_w1(0, 0, t)
-        w1_raw[0, 1] = load_w1(0, 1, "stream_b")
+        w1_second = held([P, 2, PACK, PASS], F32, "w1_second", "stream_b")
+        for a in range(2):
+            w1_raw[a, 1] = w1_second[:, a]
+            load_w1(a, 1, w1_raw[a, 1])
 
         tanh_sb, drive_bank, h = {}, {}, {}
 
-        def turn(s):
-            for half in range(2):
-                bank = psum.tile([P, BANK], F32, name="turn_bank", tag="bank%d%d" % (s % 4, half))
-                cols = slice(half * BANK, (half + 1) * BANK)
-                for a in range(2):
-                    nc.tensor.matmul_mx(
-                        out=bank[:],
-                        lhsT=w4_codes[:, a, 2 * P * s : 2 * P * (s + 1)].bitcast(FP4X4),
-                        lhsT_scale=w4_sc[a][:, P * s : P * (s + 1)],
-                        rhs=v_words[a, half][:].bitcast(FP8X4),
-                        rhs_scale=v_scales[a][:, cols],
-                        start=(a == 0),
-                        stop=(a == 1),
-                    )
-                tanh_sb[s, half] = ring.tile([P, BANK], F32, name="tanh_sb", tag="tanh_sb", bufs=6)
-                nc.scalar.activation(tanh_sb[s, half][:], bank[:], ACT.Tanh, scale=sign[:, s : s + 1])
-
-        def drive(s):
-            b, t = divmod(s, 4)
-            for half in range(2):
-                drive_bank[s, half] = psum.tile([P, BANK], F32, name="drive_bank", tag="bank%d%d" % ((s + 2) % 4, half))
-                cols = slice(half * BANK, (half + 1) * BANK)
-                for a in range(2):
-                    nc.tensor.matmul_mx(
-                        out=drive_bank[s, half][:],
-                        lhsT=w1_codes[a, b, t][:].bitcast(FP8X4),
-                        lhsT_scale=w1_scales[a, b, t][:],
-                        rhs=v_words[a, half][:].bitcast(FP8X4),
-                        rhs_scale=v_scales[a][:, cols],
-                        start=(a == 0),
-                        stop=(a == 1),
-                    )
-
-        def combine(s):
-            h[s] = ring.tile([P, S], F32, name="h", tag="h", bufs=3)
-            for half in range(2):
-                nc.vector.scalar_tensor_tensor(
-                    h[s][:, half * BANK : (half + 1) * BANK],
-                    tanh_sb[s, half][:],
-                    sgain[:, s : s + 1],
-                    drive_bank[s, half][:],
-                    ALU.add,
-                    ALU.mult,
+        def product(bank, codes, scales, half):
+            for a in range(2):
+                nc.tensor.matmul_mx(
+                    out=bank[:],
+                    lhsT=codes[a],
+                    lhsT_scale=scales[a],
+                    rhs=v_words[a, half][:].bitcast(FP8X4),
+                    rhs_scale=v_scales[a][:, half * BANK : (half + 1) * BANK],
+                    start=(a == 0),
+                    stop=(a == 1),
                 )
+
+        def turn(s, half):
+            bank = psum.tile([P, BANK], F32, name="turn_bank", tag="bank%d%d" % (s % 4, half))
+            codes = [w4_codes[:, a, 2 * P * s : 2 * P * (s + 1)].bitcast(FP4X4) for a in range(2)]
+            product(bank, codes, [w4_sc[a][:, P * s : P * (s + 1)] for a in range(2)], half)
+            tanh_sb[s, half] = held([P, BANK], F32, "tanh_sb", "tanh%d%d" % (s % 3, half))
+            nc.scalar.activation(tanh_sb[s, half][:], bank[:], ACT.Tanh, scale=sign[:, s : s + 1])
+
+        def drive(s, half):
+            b, t = divmod(s, 4)
+            drive_bank[s, half] = psum.tile([P, BANK], F32, name="drive_bank", tag="bank%d%d" % ((s + 2) % 4, half))
+            codes = [w1_codes[a, b, t][:].bitcast(FP8X4) for a in range(2)]
+            product(drive_bank[s, half], codes, [w1_scales[a, b, t][:] for a in range(2)], half)
+
+        def combine(s, half):
+            if half == 0:
+                h[s] = ring.tile([P, S], F32, name="h", tag="h", bufs=3)
+            nc.vector.scalar_tensor_tensor(
+                h[s][:, half * BANK : (half + 1) * BANK],
+                tanh_sb[s, half][:],
+                sgain[:, s : s + 1],
+                drive_bank[s, half][:],
+                ALU.add,
+                ALU.mult,
+            )
 
         x_planes = {}
         for b in range(2):
@@ -211,7 +201,7 @@ def tile_list_leadout_handover_scores_kernel(
 
         def pick(s):
             b, t = divmod(s, 4)
-            picked2 = ring.tile([P, PICK], F32, name="picked2", tag="picked2", bufs=3)
+            picked2 = held([P, PICK], F32, "picked2", "tanh%d0" % ((s + 1) % 3))
             nc.vector.tensor_copy(picked2[:], h[s][:].indirect(pos2_sb[:]))
             nc.vector.tensor_copy(x_planes[0, b][:, t, :], h[s][:].indirect(pos1_sb[:]))
             nc.scalar.activation(x_planes[1, b][:, t, :], picked2[:], ACT.Abs, scale=gc[:, 8 + s : 9 + s])
@@ -221,8 +211,8 @@ def tile_list_leadout_handover_scores_kernel(
         def weave(side, b, copy=nc.scalar.copy):
             x_bf[side, b] = held([P, PICK, PACK], BF16, "x_bf%d%d" % (side, b))
             copy(
-                x_bf[side, b][:].rearrange("p (c i) t -> p c t i", i=4),
-                x_planes[side, b][:].rearrange("p t (c i) -> p c t i", i=4),
+                x_bf[side, b][:],
+                x_planes[side, b][:].rearrange("p t c -> p c t"),
             )
 
         def quant_x(side, b):
@@ -234,27 +224,25 @@ def tile_list_leadout_handover_scores_kernel(
                 in_=x_bf[side, b][:].rearrange("p c t -> p (c t)"),
             )
 
-        turn(0)
-        turn(1)
-        round_w1(1, 0, 0, nc.vector.tensor_copy)
-        round_w1(1, 0, 1, nc.vector.tensor_copy)
-        quant_w1(1, 0, 0)
-        quant_w1(1, 0, 1)
-        drive(0)
-        drive(1)
-        combine(0)
+        for half in range(2):
+            for s in range(2):
+                turn(s, half)
+                drive(s, half)
+        for half in range(2):
+            combine(0, half)
         for s in range(1, 8):
             nxt = s + 1
             if nxt < 8:
                 b, t = divmod(nxt, 4)
-                turn(nxt)
                 if b == 1:
-                    round_w1(0, 1, t)
-                    quant_w1(0, 1, t)
-                round_w1(1, b, t)
-                quant_w1(1, b, t)
-                drive(nxt)
-            combine(s)
+                    for a in range(2):
+                        round_w1(a, 1, t)
+                        quant_w1(a, 1, t)
+                for half in range(2):
+                    turn(nxt, half)
+                    drive(nxt, half)
+            for half in range(2):
+                combine(s, half)
             pick(s - 1)
             if s == 4:
                 weave(1, 0)
@@ -262,9 +250,9 @@ def tile_list_leadout_handover_scores_kernel(
             if s == 6:
                 quant_x(1, 0)
                 quant_x(0, 0)
-        base_sb = held([P, 4, PICK], F32, "base_sb", "stream_c")
+        base_sb = held([P, 4, PICK], F32, "base_sb", "tanh21")
         nc.sync.dma_start(base_sb[:], base.rearrange("(m p) j -> p m j", p=P))
-        fin_sb = held([P, PICK], F32, "fin_sb", "stream_b")
+        fin_sb = held([P, PICK], F32, "fin_sb", "w1_first1")
         nc.sync.dma_start(fin_sb[:], fin.partition_broadcast(P))
         pick(7)
         weave(1, 1)

@@ -120,8 +120,8 @@ def tile_list_leadout_handover_scores_kernel(
 
         def round_w1(a, b, t):
             w1_bf[a, b, t] = ring.tile([P, P, PACK], BF16, name="w1_bf", tag="w1_bf", bufs=4, align_bytes=64)
-            src = w1_raw[a, b][:].rearrange("p j (g t q) -> p t g q j", t=4, q=8)[:, t]
-            dst = w1_bf[a, b, t][:].rearrange("p (g q) j -> p g q j", q=8)
+            src = w1_raw[a, b][:].rearrange("p j (g t h i) -> p t g h j i", t=4, h=2, i=4)[:, t]
+            dst = w1_bf[a, b, t][:].rearrange("p (g h i) j -> p g h j i", h=2, i=4)
             (nc.vector.tensor_copy, nc.scalar.copy)[b](dst, src)
 
         def quant_w1(a, b, t):
@@ -157,30 +157,33 @@ def tile_list_leadout_handover_scores_kernel(
 
         tanh_sb, drive_bank, h = {}, {}, {}
 
-        def product(bank, codes, scales, half):
-            for a in range(2):
-                nc.tensor.matmul_mx(
-                    out=bank[:],
-                    lhsT=codes[a],
-                    lhsT_scale=scales[a],
-                    rhs=v_words[a, half][:].bitcast(FP8X4),
-                    rhs_scale=v_scales[a][:, half * BANK : (half + 1) * BANK],
-                    start=(a == 0),
-                    stop=(a == 1),
-                )
+        turn_bank = {}
 
-        def turn(s, half):
-            bank = psum.tile([P, BANK], F32, name="turn_bank", tag="bank%d%d" % (s % 4, half))
-            codes = [w4_codes[:, a, 2 * P * s : 2 * P * (s + 1)].bitcast(FP4X4) for a in range(2)]
-            product(bank, codes, [w4_sc[a][:, P * s : P * (s + 1)] for a in range(2)], half)
-            tanh_sb[s, half] = held([P, BANK], F32, "tanh_sb", "tanh%d%d" % (s % 3, half))
-            nc.scalar.activation(tanh_sb[s, half][:], bank[:], ACT.Tanh, scale=sign[:, s : s + 1])
+        def one_pass(bank, codes, scales, a, half):
+            nc.tensor.matmul_mx(
+                out=bank[:],
+                lhsT=codes,
+                lhsT_scale=scales,
+                rhs=v_words[a, half][:].bitcast(FP8X4),
+                rhs_scale=v_scales[a][:, half * BANK : (half + 1) * BANK],
+                start=(a == 0),
+                stop=(a == 1),
+            )
 
-        def drive(s, half):
+        def turn(s, half, a):
+            if a == 0:
+                turn_bank[s, half] = psum.tile([P, BANK], F32, name="turn_bank", tag="bank%d%d" % (s % 4, half))
+            codes = w4_codes[:, a, 2 * P * s : 2 * P * (s + 1)].bitcast(FP4X4)
+            one_pass(turn_bank[s, half], codes, w4_sc[a][:, P * s : P * (s + 1)], a, half)
+            if a == 1:
+                tanh_sb[s, half] = held([P, BANK], F32, "tanh_sb", "tanh%d%d" % (s % 3, half))
+                nc.scalar.activation(tanh_sb[s, half][:], turn_bank[s, half][:], ACT.Tanh, scale=sign[:, s : s + 1])
+
+        def drive(s, half, a):
             b, t = divmod(s, 4)
-            drive_bank[s, half] = psum.tile([P, BANK], F32, name="drive_bank", tag="bank%d%d" % ((s + 2) % 4, half))
-            codes = [w1_codes[a, b, t][:].bitcast(FP8X4) for a in range(2)]
-            product(drive_bank[s, half], codes, [w1_scales[a, b, t][:] for a in range(2)], half)
+            if a == 0:
+                drive_bank[s, half] = psum.tile([P, BANK], F32, name="drive_bank", tag="bank%d%d" % ((s + 2) % 4, half))
+            one_pass(drive_bank[s, half], w1_codes[a, b, t][:].bitcast(FP8X4), w1_scales[a, b, t][:], a, half)
 
         def combine(s, half):
             if half == 0:
@@ -208,11 +211,14 @@ def tile_list_leadout_handover_scores_kernel(
 
         x_bf, x_codes, x_scales = {}, {}, {}
 
-        def weave(side, b, copy=nc.scalar.copy):
-            x_bf[side, b] = held([P, PICK, PACK], BF16, "x_bf%d%d" % (side, b))
+        for b in range(2):
+            for side in range(2):
+                x_bf[side, b] = held([P, PICK, PACK], BF16, "x_bf%d%d" % (side, b))
+
+        def weave(side, b, cols, copy=nc.scalar.copy):
             copy(
-                x_bf[side, b][:],
-                x_planes[side, b][:].rearrange("p t c -> p c t"),
+                x_bf[side, b][:, cols, :].rearrange("p (c i) t -> p c t i", i=4),
+                x_planes[side, b][:, :, cols].rearrange("p t (c i) -> p c t i", i=4),
             )
 
         def quant_x(side, b):
@@ -224,39 +230,44 @@ def tile_list_leadout_handover_scores_kernel(
                 in_=x_bf[side, b][:].rearrange("p c t -> p (c t)"),
             )
 
-        for half in range(2):
+        for a in range(2):
             for s in range(2):
-                turn(s, half)
-                drive(s, half)
+                for half in range(2):
+                    turn(s, half, a)
+                    drive(s, half, a)
         for half in range(2):
             combine(0, half)
+        low, high, whole = slice(0, PICK // 2), slice(PICK // 2, PICK), slice(0, PICK)
+        second = [(a, t) for t in range(4) for a in range(2)]
+        rounds = {1: second[0:2], 2: second[2:5], 3: second[5:8]}
+        weaves = {4: [(0, low)], 5: [(0, high), (1, low)], 6: [(1, high)]}
         for s in range(1, 8):
-            nxt = s + 1
-            if nxt < 8:
-                b, t = divmod(nxt, 4)
-                if b == 1:
-                    for a in range(2):
-                        round_w1(a, 1, t)
-                        quant_w1(a, 1, t)
+            for a, t in rounds.get(s, []):
+                round_w1(a, 1, t)
+                quant_w1(a, 1, t)
+            if s + 1 < 8:
                 for half in range(2):
-                    turn(nxt, half)
-                    drive(nxt, half)
+                    for a in range(2):
+                        turn(s + 1, half, a)
+                    for a in range(2):
+                        drive(s + 1, half, a)
             for half in range(2):
                 combine(s, half)
             pick(s - 1)
-            if s == 4:
-                weave(1, 0)
-                weave(0, 0)
+            for side, cols in weaves.get(s, []):
+                weave(side, 0, cols)
             if s == 6:
-                quant_x(1, 0)
                 quant_x(0, 0)
-        base_sb = held([P, 4, PICK], F32, "base_sb", "tanh21")
-        nc.sync.dma_start(base_sb[:], base.rearrange("(m p) j -> p m j", p=P))
-        fin_sb = held([P, PICK], F32, "fin_sb", "w1_first1")
-        nc.sync.dma_start(fin_sb[:], fin.partition_broadcast(P))
+            if s == 7:
+                quant_x(1, 0)
+        last_loads = held([P, 5, PICK], F32, "last_loads", "stream_b")
+        base_sb = last_loads[:, 0:4, :]
+        fin_sb = last_loads[:, 4, :]
+        nc.sync.dma_start(base_sb, base.rearrange("(m p) j -> p m j", p=P))
+        nc.sync.dma_start(fin_sb, fin.partition_broadcast(P))
         pick(7)
-        weave(1, 1)
-        weave(0, 1, nc.vector.tensor_copy)
+        weave(1, 1, whole)
+        weave(0, 1, whole, nc.vector.tensor_copy)
         quant_x(0, 1)
         quant_x(1, 1)
 
@@ -283,5 +294,5 @@ def tile_list_leadout_handover_scores_kernel(
 
 def finish(nc, held, total, fin_sb, out, m):
     result = held([P, PICK], F32, "result%d" % m)
-    nc.vector.tensor_tensor(result[:], total[:], fin_sb[:], ALU.mult)
+    nc.vector.tensor_tensor(result[:], total[:], fin_sb, ALU.mult)
     nc.sync.dma_start(out[P * m : P * (m + 1), :], result[:])

@@ -18,9 +18,19 @@ ALU = mybir.AluOpType
 ACT = mybir.ActivationFunctionType
 
 P = 128
-PASS = 512
-BANK = 512
 PACK = 4
+PASS = P * PACK
+BANK = 512
+SLOTS = H // P
+LIST_ROWS = 16
+SCALE_ROWS = 16
+W1_RAW_BYTES = PACK * PASS * 4
+W1_BF_BYTES = P * PACK * 2
+TANH_BYTES = BANK * 4
+W1_BF_BUFS = 4
+TANH_BUFS = 3
+H_BUFS = 3
+BANK_RING = 4
 
 
 def tile_list_leadout_handover_scores_kernel(
@@ -31,97 +41,117 @@ def tile_list_leadout_handover_scores_kernel(
         lists = ctx.enter_context(tc.tile_pool(name="lists", bufs=1))
         keep = ctx.enter_context(tc.tile_pool(name="keep", bufs=1))
         ring = ctx.enter_context(tc.tile_pool(name="ring", bufs=2))
+        shared = ctx.enter_context(tc.tile_pool(name="shared", bufs=1))
+        late = ctx.enter_context(tc.tile_pool(name="late", bufs=1))
         psum = ctx.enter_context(tc.psum_pool(name="psum", bufs=1))
 
-        offs_sb = lists.tile([P, S // 16], U16, name="offs_sb")
-        pos1_sb = lists.tile([P, PICK // 16], U16, name="pos1_sb")
-        pos2_sb = lists.tile([P, PICK // 16], U16, name="pos2_sb")
+        offs_sb = lists.tile([P, S // LIST_ROWS], U16, name="offs_sb")
+        pos1_sb = lists.tile([P, PICK // LIST_ROWS], U16, name="pos1_sb")
+        pos2_sb = lists.tile([P, PICK // LIST_ROWS], U16, name="pos2_sb")
 
         def held(shape, dtype, name, tag=None):
             return keep.tile(shape, dtype, name=name, tag=tag or name, align_bytes=64)
 
+        def bank_tag(place, half):
+            return "bank%d%d" % (place % BANK_RING, half)
+
         nc.sync.dma_start(offs_sb[:], offs)
         scale_rows = held([P, T], U8, "scale_rows")
         nc.sync.dma_start(
-            scale_rows[0:32, :].bitcast(I32), tab_scales.rearrange("a q t -> (a q) t").bitcast(I32)
+            scale_rows[0 : 2 * SCALE_ROWS, :].bitcast(I32), tab_scales.rearrange("a q t -> (a q) t").bitcast(I32)
         )
-        w4_rows = held([32, H], U8, "w4_rows")
+        w4_rows = held([2 * SCALE_ROWS, H], U8, "w4_rows")
         nc.sync.dma_start(w4_rows[:].bitcast(I32), w4_scales.rearrange("a q c -> (a q) c").bitcast(I32))
+        gc_raw = held([4, PASS], F32, "gc_raw")
+        for v, vec in enumerate((gain, chan)):
+            nc.sync.dma_start(gc_raw[2 * v : 2 * v + 2, :], vec.rearrange("(b c) -> b c", b=2))
 
-        def load_table(a, tag):
-            words = held([P, T], U32, "tab_words%d" % a, tag)
+        def load_table(a, words):
             nc.sync.dma_start(words[:].bitcast(I32), tab_words[a].rearrange("p t i -> p (t i)").bitcast(I32))
-            return words
 
         def load_w1(a, b, raw):
             rows = w1[PASS * a : PASS * (a + 1), PASS * b : PASS * (b + 1)]
             nc.sync.dma_start(raw, rows.rearrange("(p j) c -> p j c", j=PACK))
 
-        table0 = load_table(0, "stream_a")
+        table0 = held([P, T], U32, "table0")
+        load_table(0, table0)
         w4_raw = held([P, 2, 2 * H], U8, "w4_raw")
         nc.sync.dma_start(w4_raw[:].bitcast(I32), w4_words.rearrange("a p c -> p a c").bitcast(I32))
         nc.sync.dma_start(pos1_sb[:], pos1)
         nc.sync.dma_start(pos2_sb[:], pos2)
 
-        rows_gc = held([P, 2 * P], F32, "rows_gc")
+        rows_gc = held([P, PASS], F32, "rows_gc")
         nc.gpsimd.memset(rows_gc[:], 0.0)
+        nc.scalar.copy(
+            rows_gc[0:4, :].rearrange("r (t g q) -> r t g q", t=PACK, q=8),
+            gc_raw[:].rearrange("r (g t q) -> r t g q", t=PACK, q=8),
+        )
         nc.vector.memset(scale_rows[32:64, :].bitcast(I32), 0)
         nc.vector.memset(scale_rows[64:128, :].bitcast(I32), 0)
         planes = held([P, 2, S + H], U8, "planes")
         nc.gpsimd.memset(planes[:].bitcast(I32), 0)
         v_scales = [planes[:, a, 0:S] for a in range(2)]
         w4_sc = [planes[:, a, S : S + H] for a in range(2)]
-        for v, vec in enumerate((gain, chan)):
-            nc.sync.dma_start(
-                rows_gc[4 * v : 4 * v + 4, :].rearrange("t (g q) -> t g q", q=8),
-                vec.rearrange("(g t q) -> t g q", t=4, q=8),
-            )
-        w1_raw = {(a, 0): held([P, PACK, PASS], F32, "w1_first%d" % a) for a in range(2)}
-        for a in range(2):
-            load_w1(a, 0, w1_raw[a, 0][:])
-        table1 = load_table(1, "stream_b")
+        w1_raw = {(0, 0): held([P, PACK, PASS], F32, "w1_first0")}
+        load_w1(0, 0, w1_raw[0, 0][:])
         ident = held([P, P], F32, "ident")
         make_identity(nc, ident[:])
 
-        picked_rows = held([P, S], U8, "picked_rows")
-        staged = held([32, 2, S + H], U8, "staged")
+        picked_rows = late.tile([P, S], U8, name="picked_rows", offset=W1_RAW_BYTES - S // 2, align_bytes=64)
+        staged = held([2 * SCALE_ROWS, 2, S + H], U8, "staged")
         nc.vector.tensor_copy(picked_rows[:], scale_rows[:].indirect(offs_sb[:]))
         nc.vector.tensor_copy(
-            staged[:, 0, S : S + H].bitcast(I32).rearrange("p (b t g w) -> p b t g w", b=2, t=4, w=2),
-            w4_rows[:].bitcast(I32).rearrange("p (b g t w) -> p b t g w", b=2, t=4, w=2),
+            staged[:, 0, S : S + H].bitcast(I32).rearrange("p (b t g w) -> p b t g w", b=2, t=PACK, w=2),
+            w4_rows[:].bitcast(I32).rearrange("p (b g t w) -> p b t g w", b=2, t=PACK, w=2),
         )
-        nc.vector.tensor_copy(staged[:, 0, 0:S].bitcast(I32), picked_rows[0:32, :].bitcast(I32))
-        nc.scalar.dma_start(staged[0:16, 1, :].bitcast(I32), staged[16:32, 0, :].bitcast(I32))
-        for q in range(4):
+        nc.vector.tensor_copy(staged[:, 0, 0:S].bitcast(I32), picked_rows[0 : 2 * SCALE_ROWS, :].bitcast(I32))
+        nc.scalar.dma_start(
+            staged[0:SCALE_ROWS, 1, :].bitcast(I32), staged[SCALE_ROWS : 2 * SCALE_ROWS, 0, :].bitcast(I32)
+        )
+        w1_raw[1, 0] = late.tile([P, PACK, PASS], F32, name="w1_first1", offset=0, align_bytes=64)
+        load_w1(1, 0, w1_raw[1, 0][:])
+        table1 = late.tile([P, T], U32, name="table1", offset=W1_RAW_BYTES, align_bytes=64)
+        load_table(1, table1)
+        for quadrant in range(4):
             nc.scalar.dma_start(
-                planes[32 * q : 32 * q + 4, :, :].bitcast(I32), staged[4 * q : 4 * q + 4, :, :].bitcast(I32)
+                planes[32 * quadrant : 32 * quadrant + 4, :, :].bitcast(I32),
+                staged[4 * quadrant : 4 * quadrant + 4, :, :].bitcast(I32),
             )
 
-        gc_bank = psum.tile([P, 2, P], F32, name="gc_bank", tag="bank30")
-        for b in range(2):
-            nc.tensor.transpose(gc_bank[:, b, :], rows_gc[:, P * b : P * (b + 1)], ident[:])
-        gc = held([P, 16], F32, "gc")
-        nc.scalar.copy(
-            gc[:].rearrange("p (v b t) -> p v b t", v=2, b=2),
-            gc_bank[:, :, 0:8].rearrange("p b (v t) -> p v b t", v=2),
+        gc_bank = psum.tile([P, PACK, P], F32, name="gc_bank", tag=bank_tag(3, 0))
+        for t in range(PACK):
+            nc.tensor.transpose(gc_bank[:, t, :], rows_gc[:, P * t : P * (t + 1)], ident[:])
+        gc = held([P, 2 * SLOTS], F32, "gc")
+        nc.scalar.activation(
+            gc[:].rearrange("p (r t) -> p r t", t=PACK),
+            gc_bank[:, :, 0:4].rearrange("p t r -> p r t"),
+            ACT.Copy,
         )
-        step01 = held([P, 8], F32, "step01")
-        sign = held([P, 8], F32, "sign")
-        sgain = held([P, 8], F32, "sgain")
+        twice_step = held([P, SLOTS], F32, "step01")
+        sign = held([P, SLOTS], F32, "sign")
+        sgain = held([P, SLOTS], F32, "sgain")
 
         v_words = {}
 
         def gather_words(a, half, table):
             v_words[a, half] = held([P, BANK], U32, "v_words%d%d" % (a, half))
-            cols = slice(half * BANK // 16, (half + 1) * BANK // 16)
+            cols = slice(half * BANK // LIST_ROWS, (half + 1) * BANK // LIST_ROWS)
             nc.vector.tensor_copy(v_words[a, half][:], table[:].indirect(offs_sb[:, cols]))
 
         w1_bf, w1_codes, w1_scales = {}, {}, {}
 
         def round_w1(a, b, t):
-            w1_bf[a, b, t] = ring.tile([P, P, PACK], BF16, name="w1_bf", tag="w1_bf", bufs=4, align_bytes=64)
-            src = w1_raw[a, b][:].rearrange("p j (g t h i) -> p t g h j i", t=4, h=2, i=4)[:, t]
-            dst = w1_bf[a, b, t][:].rearrange("p (g h i) j -> p g h j i", h=2, i=4)
+            if b == 0:
+                w1_bf[a, b, t] = ring.tile(
+                    [P, P, PACK], BF16, name="w1_bf", tag="w1_bf", bufs=W1_BF_BUFS, align_bytes=64
+                )
+            else:
+                place = W1_BF_BYTES * ((2 * t + a) % W1_BF_BUFS)
+                w1_bf[a, b, t] = shared.tile(
+                    [P, P, PACK], BF16, name="w1_late%d%d" % (a, t), offset=place, align_bytes=64
+                )
+            src = w1_raw[a, b][:].rearrange("p j (g t u i) -> p t g u j i", t=PACK, u=2, i=4)[:, t]
+            dst = w1_bf[a, b, t][:].rearrange("p (g u i) j -> p g u j i", u=2, i=4)
             (nc.vector.tensor_copy, nc.scalar.copy)[b](dst, src)
 
         def quant_w1(a, b, t):
@@ -137,27 +167,26 @@ def tile_list_leadout_handover_scores_kernel(
         gather_words(0, 1, table0)
         w4_codes = held([P, 2, 2 * H], U8, "w4_codes")
         nc.vector.tensor_copy(
-            w4_codes[:].bitcast(I32).rearrange("p a (b t g w) -> p (a b) t g w", b=2, t=4, w=4),
-            w4_raw[:].bitcast(I32).rearrange("p a (b g t w) -> p (a b) t g w", b=2, t=4, w=4),
+            w4_codes[:].bitcast(I32).rearrange("p a (b t g w) -> p (a b) t g w", b=2, t=PACK, w=4),
+            w4_raw[:].bitcast(I32).rearrange("p a (b g t w) -> p (a b) t g w", b=2, t=PACK, w=4),
         )
-        nc.vector.tensor_scalar(step01[:], gc[:, 8:16], 0.0, 2.0, ALU.is_ge, ALU.mult)
-        nc.vector.tensor_scalar(sign[:], step01[:], -1.0, None, ALU.add)
-        nc.vector.tensor_tensor(sgain[:], gc[:, 0:8], sign[:], ALU.mult)
+        nc.vector.tensor_scalar(twice_step[:], gc[:, SLOTS : 2 * SLOTS], 0.0, 2.0, ALU.is_ge, ALU.mult)
+        nc.vector.tensor_scalar(sign[:], twice_step[:], -1.0, None, ALU.add)
+        nc.vector.tensor_tensor(sgain[:], gc[:, 0:SLOTS], sign[:], ALU.mult)
         for a in range(2):
-            for t in range(4):
+            for t in range(PACK):
                 round_w1(a, 0, t)
-            for t in range(4):
+            for t in range(PACK):
                 quant_w1(a, 0, t)
+            if a == 0:
+                w1_raw[a, 1] = held([P, PACK, PASS], F32, "w1_second0", "w1_first0")
+            else:
+                w1_raw[a, 1] = late.tile([P, PACK, PASS], F32, name="w1_second1", offset=0, align_bytes=64)
+            load_w1(a, 1, w1_raw[a, 1][:])
         gather_words(1, 0, table1)
         gather_words(1, 1, table1)
-        w1_second = held([P, 2, PACK, PASS], F32, "w1_second", "stream_b")
-        for a in range(2):
-            w1_raw[a, 1] = w1_second[:, a]
-            load_w1(a, 1, w1_raw[a, 1])
 
-        tanh_sb, drive_bank, h = {}, {}, {}
-
-        turn_bank = {}
+        turn_bank, drive_bank, tanh_sb, h = {}, {}, {}, {}
 
         def one_pass(bank, codes, scales, a, half):
             nc.tensor.matmul_mx(
@@ -172,22 +201,27 @@ def tile_list_leadout_handover_scores_kernel(
 
         def turn(s, half, a):
             if a == 0:
-                turn_bank[s, half] = psum.tile([P, BANK], F32, name="turn_bank", tag="bank%d%d" % (s % 4, half))
+                turn_bank[s, half] = psum.tile([P, BANK], F32, name="turn_bank", tag=bank_tag(s, half))
             codes = w4_codes[:, a, 2 * P * s : 2 * P * (s + 1)].bitcast(FP4X4)
             one_pass(turn_bank[s, half], codes, w4_sc[a][:, P * s : P * (s + 1)], a, half)
             if a == 1:
-                tanh_sb[s, half] = held([P, BANK], F32, "tanh_sb", "tanh%d%d" % (s % 3, half))
+                if s == 0:
+                    tanh_sb[s, half] = shared.tile(
+                        [P, BANK], F32, name="tanh_first%d" % half, offset=TANH_BYTES * half, align_bytes=64
+                    )
+                else:
+                    tanh_sb[s, half] = held([P, BANK], F32, "tanh_sb", "tanh%d%d" % (s % TANH_BUFS, half))
                 nc.scalar.activation(tanh_sb[s, half][:], turn_bank[s, half][:], ACT.Tanh, scale=sign[:, s : s + 1])
 
         def drive(s, half, a):
-            b, t = divmod(s, 4)
+            b, t = divmod(s, PACK)
             if a == 0:
-                drive_bank[s, half] = psum.tile([P, BANK], F32, name="drive_bank", tag="bank%d%d" % ((s + 2) % 4, half))
+                drive_bank[s, half] = psum.tile([P, BANK], F32, name="drive_bank", tag=bank_tag(s + 2, half))
             one_pass(drive_bank[s, half], w1_codes[a, b, t][:].bitcast(FP8X4), w1_scales[a, b, t][:], a, half)
 
         def combine(s, half):
             if half == 0:
-                h[s] = ring.tile([P, S], F32, name="h", tag="h", bufs=3)
+                h[s] = ring.tile([P, S], F32, name="h", tag="h", bufs=H_BUFS)
             nc.vector.scalar_tensor_tensor(
                 h[s][:, half * BANK : (half + 1) * BANK],
                 tanh_sb[s, half][:],
@@ -197,37 +231,41 @@ def tile_list_leadout_handover_scores_kernel(
                 ALU.mult,
             )
 
-        x_planes = {}
+        x_slots = {}
         for b in range(2):
             for side in range(2):
-                x_planes[side, b] = held([P, PACK, PICK], BF16, "x_planes%d%d" % (side, b))
+                x_slots[side, b] = held([P, PACK, PICK], BF16, "x_planes%d%d" % (side, b))
 
         def pick(s):
-            b, t = divmod(s, 4)
-            picked2 = held([P, PICK], F32, "picked2", "tanh%d0" % ((s + 1) % 3))
+            b, t = divmod(s, PACK)
+            picked2 = held([P, PICK], F32, "picked2", "tanh%d0" % ((s + 1) % TANH_BUFS))
             nc.vector.tensor_copy(picked2[:], h[s][:].indirect(pos2_sb[:]))
-            nc.vector.tensor_copy(x_planes[0, b][:, t, :], h[s][:].indirect(pos1_sb[:]))
-            nc.scalar.activation(x_planes[1, b][:, t, :], picked2[:], ACT.Abs, scale=gc[:, 8 + s : 9 + s])
+            nc.vector.tensor_copy(x_slots[0, b][:, t, :], h[s][:].indirect(pos1_sb[:]))
+            nc.scalar.activation(
+                x_slots[1, b][:, t, :], picked2[:], ACT.Abs, scale=gc[:, SLOTS + s : SLOTS + s + 1]
+            )
 
         x_bf, x_codes, x_scales = {}, {}, {}
-
         for b in range(2):
             for side in range(2):
                 x_bf[side, b] = held([P, PICK, PACK], BF16, "x_bf%d%d" % (side, b))
 
-        def weave(side, b, cols, copy=nc.scalar.copy):
+        def interleave(side, b, cols, copy=nc.scalar.copy):
             copy(
                 x_bf[side, b][:, cols, :].rearrange("p (c i) t -> p c t i", i=4),
-                x_planes[side, b][:, :, cols].rearrange("p t (c i) -> p c t i", i=4),
+                x_slots[side, b][:, :, cols].rearrange("p t (c i) -> p c t i", i=4),
             )
 
-        def quant_x(side, b):
-            x_codes[side, b] = held([P, PICK], U32, "x_codes%d%d" % (side, b))
-            x_scales[side, b] = held([P, PICK], U8, "x_scales%d%d" % (side, b))
+        for b in range(2):
+            for side in range(2):
+                x_codes[side, b] = held([P, PICK], U32, "x_codes%d%d" % (side, b))
+                x_scales[side, b] = held([P, PICK], U8, "x_scales%d%d" % (side, b))
+
+        def quant_x(side, b, cols):
             nc.vector.quantize_mx(
-                out=x_codes[side, b][:].bitcast(FP8X4),
-                scales=x_scales[side, b][:],
-                in_=x_bf[side, b][:].rearrange("p c t -> p (c t)"),
+                out=x_codes[side, b][:, cols].bitcast(FP8X4),
+                scales=x_scales[side, b][:, cols],
+                in_=x_bf[side, b][:, cols, :].rearrange("p c t -> p (c t)"),
             )
 
         for a in range(2):
@@ -238,14 +276,15 @@ def tile_list_leadout_handover_scores_kernel(
         for half in range(2):
             combine(0, half)
         low, high, whole = slice(0, PICK // 2), slice(PICK // 2, PICK), slice(0, PICK)
-        second = [(a, t) for t in range(4) for a in range(2)]
+        second = [(a, t) for t in range(PACK) for a in range(2)]
         rounds = {1: second[0:2], 2: second[2:5], 3: second[5:8]}
-        weaves = {4: [(0, low)], 5: [(0, high), (1, low)], 6: [(1, high)]}
-        for s in range(1, 8):
+        halves = {4: [(0, low)], 5: [(0, high), (1, low)], 6: [(1, high)]}
+        quantise_after = {6: 0, 7: 1}
+        for s in range(1, SLOTS):
             for a, t in rounds.get(s, []):
                 round_w1(a, 1, t)
                 quant_w1(a, 1, t)
-            if s + 1 < 8:
+            if s + 1 < SLOTS:
                 for half in range(2):
                     for a in range(2):
                         turn(s + 1, half, a)
@@ -254,26 +293,26 @@ def tile_list_leadout_handover_scores_kernel(
             for half in range(2):
                 combine(s, half)
             pick(s - 1)
-            for side, cols in weaves.get(s, []):
-                weave(side, 0, cols)
-            if s == 6:
-                quant_x(0, 0)
-            if s == 7:
-                quant_x(1, 0)
-        last_loads = held([P, 5, PICK], F32, "last_loads", "stream_b")
+            for side, cols in halves.get(s, []):
+                interleave(side, 0, cols)
+            if s in quantise_after:
+                quant_x(quantise_after[s], 0, whole)
+        last_loads = held([P, 5, PICK], F32, "last_loads", "w1_first0")
         base_sb = last_loads[:, 0:4, :]
         fin_sb = last_loads[:, 4, :]
         nc.sync.dma_start(base_sb, base.rearrange("(m p) j -> p m j", p=P))
         nc.sync.dma_start(fin_sb, fin.partition_broadcast(P))
-        pick(7)
-        weave(1, 1, whole)
-        weave(0, 1, whole, nc.vector.tensor_copy)
-        quant_x(0, 1)
-        quant_x(1, 1)
+        pick(SLOTS - 1)
+        interleave(1, 1, whole)
+        interleave(0, 1, low, nc.vector.tensor_copy)
+        interleave(0, 1, high, nc.vector.tensor_copy)
+        quant_x(0, 1, low)
+        quant_x(1, 1, whole)
+        quant_x(0, 1, high)
 
-        sums = []
-        for m in range(4):
-            bank = psum.tile([P, PICK], F32, name="score_bank", tag="bank%d%d" % (2 + m // 2, m % 2))
+        totals = []
+        for m in range(PICK // P):
+            bank = psum.tile([P, PICK], F32, name="score_bank", tag=bank_tag(2 + m // 2, m % 2))
             for b in range(2):
                 nc.tensor.matmul_mx(
                     out=bank[:],
@@ -284,15 +323,10 @@ def tile_list_leadout_handover_scores_kernel(
                     start=(b == 0),
                     stop=(b == 1),
                 )
-            total = held([P, PICK], F32, "total%d" % m)
-            nc.vector.tensor_tensor(total[:], bank[:], base_sb[:, m, :], ALU.add)
-            sums.append(total)
-            if m > 0:
-                finish(nc, held, sums[m - 1], fin_sb, out, m - 1)
-        finish(nc, held, sums[3], fin_sb, out, 3)
-
-
-def finish(nc, held, total, fin_sb, out, m):
-    result = held([P, PICK], F32, "result%d" % m)
-    nc.vector.tensor_tensor(result[:], total[:], fin_sb, ALU.mult)
-    nc.sync.dma_start(out[P * m : P * (m + 1), :], result[:])
+            totals.append(held([P, PICK], F32, "total%d" % m))
+            nc.vector.tensor_tensor(totals[m][:], bank[:], base_sb[:, m, :], ALU.add)
+        for m in range(PICK // P):
+            result = held([P, PICK], F32, "result%d" % m)
+            engine = nc.gpsimd if m == 0 else nc.vector
+            engine.tensor_tensor(result[:], totals[m][:], fin_sb, ALU.mult)
+            nc.sync.dma_start(out[P * m : P * (m + 1), :], result[:])

from contextlib import ExitStack

import concourse.mybir as mybir
from concourse.masks import make_identity

K, H, T, S, PICK = 1024, 1024, 4096, 1024, 512
FLOPS = 2 * (2 * K * H * S + H * PICK * PICK)

F32 = mybir.dt.float32
BF16 = mybir.dt.bfloat16
I32 = mybir.dt.int32
U32 = mybir.dt.uint32
U16 = mybir.dt.uint16
U8 = mybir.dt.uint8
FP8X4 = mybir.dt.float8_e4m3fn_x4
FP4X4 = mybir.dt.float4_e2m1fn_x4
ALU = mybir.AluOpType
ACT = mybir.ActivationFunctionType

P = 128
PACK = 4
PASS = P * PACK
BANK = 512
SLOTS = H // P
LIST_ROWS = 16
SCALE_ROWS = 16
W1_RAW_BYTES = PACK * PASS * 4
W1_BF_BYTES = P * PACK * 2
TANH_BYTES = BANK * 4
W1_BF_BUFS = 4
TANH_BUFS = 3
H_BUFS = 3
BANK_RING = 4


def tile_list_leadout_handover_scores_kernel(
    tc, tab_words, tab_scales, offs, pos1, pos2, w1, w4_words, w4_scales, gain, chan, base, fin, out
):
    nc = tc.nc
    with ExitStack() as ctx:
        lists = ctx.enter_context(tc.tile_pool(name="lists", bufs=1))
        keep = ctx.enter_context(tc.tile_pool(name="keep", bufs=1))
        ring = ctx.enter_context(tc.tile_pool(name="ring", bufs=2))
        shared = ctx.enter_context(tc.tile_pool(name="shared", bufs=1))
        late = ctx.enter_context(tc.tile_pool(name="late", bufs=1))
        psum = ctx.enter_context(tc.psum_pool(name="psum", bufs=1))

        offs_sb = lists.tile([P, S // LIST_ROWS], U16, name="offs_sb")
        pos1_sb = lists.tile([P, PICK // LIST_ROWS], U16, name="pos1_sb")
        pos2_sb = lists.tile([P, PICK // LIST_ROWS], U16, name="pos2_sb")

        def held(shape, dtype, name, tag=None):
            return keep.tile(shape, dtype, name=name, tag=tag or name, align_bytes=64)

        def bank_tag(place, half):
            return "bank%d%d" % (place % BANK_RING, half)

        nc.sync.dma_start(offs_sb[:], offs)
        scale_rows = held([P, T], U8, "scale_rows")
        nc.sync.dma_start(
            scale_rows[0 : 2 * SCALE_ROWS, :].bitcast(I32), tab_scales.rearrange("a q t -> (a q) t").bitcast(I32)
        )
        w4_rows = held([2 * SCALE_ROWS, H], U8, "w4_rows")
        nc.sync.dma_start(w4_rows[:].bitcast(I32), w4_scales.rearrange("a q c -> (a q) c").bitcast(I32))
        gc_raw = held([4, PASS], F32, "gc_raw")
        for v, vec in enumerate((gain, chan)):
            nc.sync.dma_start(gc_raw[2 * v : 2 * v + 2, :], vec.rearrange("(b c) -> b c", b=2))

        def load_table(a, words):
            nc.sync.dma_start(words[:].bitcast(I32), tab_words[a].rearrange("p t i -> p (t i)").bitcast(I32))

        def load_w1(a, b, raw):
            rows = w1[PASS * a : PASS * (a + 1), PASS * b : PASS * (b + 1)]
            nc.sync.dma_start(raw, rows.rearrange("(p j) c -> p j c", j=PACK))

        table0 = held([P, T], U32, "table0")
        load_table(0, table0)
        w4_raw = held([P, 2, 2 * H], U8, "w4_raw")
        nc.sync.dma_start(w4_raw[:].bitcast(I32), w4_words.rearrange("a p c -> p a c").bitcast(I32))
        nc.sync.dma_start(pos1_sb[:], pos1)
        nc.sync.dma_start(pos2_sb[:], pos2)

        rows_gc = held([P, PASS], F32, "rows_gc")
        nc.gpsimd.memset(rows_gc[:], 0.0)
        nc.scalar.copy(
            rows_gc[0:4, :].rearrange("r (t g q) -> r t g q", t=PACK, q=8),
            gc_raw[:].rearrange("r (g t q) -> r t g q", t=PACK, q=8),
        )
        nc.vector.memset(scale_rows[32:64, :].bitcast(I32), 0)
        nc.vector.memset(scale_rows[64:128, :].bitcast(I32), 0)
        planes = held([P, 2, S + H], U8, "planes")
        nc.gpsimd.memset(planes[:].bitcast(I32), 0)
        v_scales = [planes[:, a, 0:S] for a in range(2)]
        w4_sc = [planes[:, a, S : S + H] for a in range(2)]
        w1_raw = {(0, 0): held([P, PACK, PASS], F32, "w1_first0")}
        load_w1(0, 0, w1_raw[0, 0][:])
        ident = held([P, P], F32, "ident")
        make_identity(nc, ident[:])

        picked_rows = late.tile([P, S], U8, name="picked_rows", offset=W1_RAW_BYTES - S // 2, align_bytes=64)
        staged = held([2 * SCALE_ROWS, 2, S + H], U8, "staged")
        nc.vector.tensor_copy(picked_rows[:], scale_rows[:].indirect(offs_sb[:]))
        nc.vector.tensor_copy(
            staged[:, 0, S : S + H].bitcast(I32).rearrange("p (b t g w) -> p b t g w", b=2, t=PACK, w=2),
            w4_rows[:].bitcast(I32).rearrange("p (b g t w) -> p b t g w", b=2, t=PACK, w=2),
        )
        nc.vector.tensor_copy(staged[:, 0, 0:S].bitcast(I32), picked_rows[0 : 2 * SCALE_ROWS, :].bitcast(I32))
        nc.scalar.dma_start(
            staged[0:SCALE_ROWS, 1, :].bitcast(I32), staged[SCALE_ROWS : 2 * SCALE_ROWS, 0, :].bitcast(I32)
        )
        w1_raw[1, 0] = late.tile([P, PACK, PASS], F32, name="w1_first1", offset=0, align_bytes=64)
        load_w1(1, 0, w1_raw[1, 0][:])
        table1 = late.tile([P, T], U32, name="table1", offset=W1_RAW_BYTES, align_bytes=64)
        load_table(1, table1)
        for quadrant in range(4):
            nc.scalar.dma_start(
                planes[32 * quadrant : 32 * quadrant + 4, :, :].bitcast(I32),
                staged[4 * quadrant : 4 * quadrant + 4, :, :].bitcast(I32),
            )

        gc_bank = psum.tile([P, PACK, P], F32, name="gc_bank", tag=bank_tag(3, 0))
        for t in range(PACK):
            nc.tensor.transpose(gc_bank[:, t, :], rows_gc[:, P * t : P * (t + 1)], ident[:])
        gc = held([P, 2 * SLOTS], F32, "gc")
        nc.scalar.activation(
            gc[:].rearrange("p (r t) -> p r t", t=PACK),
            gc_bank[:, :, 0:4].rearrange("p t r -> p r t"),
            ACT.Copy,
        )
        twice_step = held([P, SLOTS], F32, "step01")
        sign = held([P, SLOTS], F32, "sign")
        sgain = held([P, SLOTS], F32, "sgain")

        v_words = {}

        def gather_words(a, half, table):
            v_words[a, half] = held([P, BANK], U32, "v_words%d%d" % (a, half))
            cols = slice(half * BANK // LIST_ROWS, (half + 1) * BANK // LIST_ROWS)
            nc.vector.tensor_copy(v_words[a, half][:], table[:].indirect(offs_sb[:, cols]))

        w1_bf, w1_codes, w1_scales = {}, {}, {}

        def round_w1(a, b, t):
            if b == 0:
                w1_bf[a, b, t] = ring.tile(
                    [P, P, PACK], BF16, name="w1_bf", tag="w1_bf", bufs=W1_BF_BUFS, align_bytes=64
                )
            else:
                place = W1_BF_BYTES * ((2 * t + a) % W1_BF_BUFS)
                w1_bf[a, b, t] = shared.tile(
                    [P, P, PACK], BF16, name="w1_late%d%d" % (a, t), offset=place, align_bytes=64
                )
            src = w1_raw[a, b][:].rearrange("p j (g t u i) -> p t g u j i", t=PACK, u=2, i=4)[:, t]
            dst = w1_bf[a, b, t][:].rearrange("p (g u i) j -> p g u j i", u=2, i=4)
            (nc.vector.tensor_copy, nc.scalar.copy)[b](dst, src)

        def quant_w1(a, b, t):
            w1_codes[a, b, t] = held([P, P], U32, "w1_codes%d%d%d" % (a, b, t))
            w1_scales[a, b, t] = held([P, P], U8, "w1_scales%d%d%d" % (a, b, t))
            nc.vector.quantize_mx(
                out=w1_codes[a, b, t][:].bitcast(FP8X4),
                scales=w1_scales[a, b, t][:],
                in_=w1_bf[a, b, t][:].rearrange("p c j -> p (c j)"),
            )

        gather_words(0, 0, table0)
        gather_words(0, 1, table0)
        w4_codes = held([P, 2, 2 * H], U8, "w4_codes")
        nc.vector.tensor_copy(
            w4_codes[:].bitcast(I32).rearrange("p a (b t g w) -> p (a b) t g w", b=2, t=PACK, w=4),
            w4_raw[:].bitcast(I32).rearrange("p a (b g t w) -> p (a b) t g w", b=2, t=PACK, w=4),
        )
        nc.vector.tensor_scalar(twice_step[:], gc[:, SLOTS : 2 * SLOTS], 0.0, 2.0, ALU.is_ge, ALU.mult)
        nc.vector.tensor_scalar(sign[:], twice_step[:], -1.0, None, ALU.add)
        nc.vector.tensor_tensor(sgain[:], gc[:, 0:SLOTS], sign[:], ALU.mult)
        for a in range(2):
            for t in range(PACK):
                round_w1(a, 0, t)
            for t in range(PACK):
                quant_w1(a, 0, t)
            if a == 0:
                w1_raw[a, 1] = held([P, PACK, PASS], F32, "w1_second0", "w1_first0")
            else:
                w1_raw[a, 1] = late.tile([P, PACK, PASS], F32, name="w1_second1", offset=0, align_bytes=64)
            load_w1(a, 1, w1_raw[a, 1][:])
        gather_words(1, 0, table1)
        gather_words(1, 1, table1)

        turn_bank, drive_bank, tanh_sb, h = {}, {}, {}, {}

        def one_pass(bank, codes, scales, a, half):
            nc.tensor.matmul_mx(
                out=bank[:],
                lhsT=codes,
                lhsT_scale=scales,
                rhs=v_words[a, half][:].bitcast(FP8X4),
                rhs_scale=v_scales[a][:, half * BANK : (half + 1) * BANK],
                start=(a == 0),
                stop=(a == 1),
            )

        def turn(s, half, a):
            if a == 0:
                turn_bank[s, half] = psum.tile([P, BANK], F32, name="turn_bank", tag=bank_tag(s, half))
            codes = w4_codes[:, a, 2 * P * s : 2 * P * (s + 1)].bitcast(FP4X4)
            one_pass(turn_bank[s, half], codes, w4_sc[a][:, P * s : P * (s + 1)], a, half)
            if a == 1:
                if s == 0:
                    tanh_sb[s, half] = shared.tile(
                        [P, BANK], F32, name="tanh_first%d" % half, offset=TANH_BYTES * half, align_bytes=64
                    )
                else:
                    tanh_sb[s, half] = held([P, BANK], F32, "tanh_sb", "tanh%d%d" % (s % TANH_BUFS, half))
                nc.scalar.activation(tanh_sb[s, half][:], turn_bank[s, half][:], ACT.Tanh, scale=sign[:, s : s + 1])

        def drive(s, half, a):
            b, t = divmod(s, PACK)
            if a == 0:
                drive_bank[s, half] = psum.tile([P, BANK], F32, name="drive_bank", tag=bank_tag(s + 2, half))
            one_pass(drive_bank[s, half], w1_codes[a, b, t][:].bitcast(FP8X4), w1_scales[a, b, t][:], a, half)

        def combine(s, half):
            if half == 0:
                h[s] = ring.tile([P, S], F32, name="h", tag="h", bufs=H_BUFS)
            nc.vector.scalar_tensor_tensor(
                h[s][:, half * BANK : (half + 1) * BANK],
                tanh_sb[s, half][:],
                sgain[:, s : s + 1],
                drive_bank[s, half][:],
                ALU.add,
                ALU.mult,
            )

        x_slots = {}
        for b in range(2):
            for side in range(2):
                x_slots[side, b] = held([P, PACK, PICK], BF16, "x_planes%d%d" % (side, b))

        def pick(s):
            b, t = divmod(s, PACK)
            picked2 = held([P, PICK], F32, "picked2", "tanh%d0" % ((s + 1) % TANH_BUFS))
            nc.vector.tensor_copy(picked2[:], h[s][:].indirect(pos2_sb[:]))
            nc.vector.tensor_copy(x_slots[0, b][:, t, :], h[s][:].indirect(pos1_sb[:]))
            nc.scalar.activation(
                x_slots[1, b][:, t, :], picked2[:], ACT.Abs, scale=gc[:, SLOTS + s : SLOTS + s + 1]
            )

        x_bf, x_codes, x_scales = {}, {}, {}
        for b in range(2):
            for side in range(2):
                x_bf[side, b] = held([P, PICK, PACK], BF16, "x_bf%d%d" % (side, b))

        def interleave(side, b, cols, copy=nc.scalar.copy):
            copy(
                x_bf[side, b][:, cols, :].rearrange("p (c i) t -> p c t i", i=4),
                x_slots[side, b][:, :, cols].rearrange("p t (c i) -> p c t i", i=4),
            )

        for b in range(2):
            for side in range(2):
                x_codes[side, b] = held([P, PICK], U32, "x_codes%d%d" % (side, b))
                x_scales[side, b] = held([P, PICK], U8, "x_scales%d%d" % (side, b))

        def quant_x(side, b, cols):
            nc.vector.quantize_mx(
                out=x_codes[side, b][:, cols].bitcast(FP8X4),
                scales=x_scales[side, b][:, cols],
                in_=x_bf[side, b][:, cols, :].rearrange("p c t -> p (c t)"),
            )

        for a in range(2):
            for s in range(2):
                for half in range(2):
                    turn(s, half, a)
                    drive(s, half, a)
        for half in range(2):
            combine(0, half)
        low, high, whole = slice(0, PICK // 2), slice(PICK // 2, PICK), slice(0, PICK)
        second = [(a, t) for t in range(PACK) for a in range(2)]
        rounds = {1: second[0:2], 2: second[2:5], 3: second[5:8]}
        halves = {4: [(0, low)], 5: [(0, high), (1, low)], 6: [(1, high)]}
        quantise_after = {6: 0, 7: 1}
        for s in range(1, SLOTS):
            for a, t in rounds.get(s, []):
                round_w1(a, 1, t)
                quant_w1(a, 1, t)
            if s + 1 < SLOTS:
                for half in range(2):
                    for a in range(2):
                        turn(s + 1, half, a)
                    for a in range(2):
                        drive(s + 1, half, a)
            for half in range(2):
                combine(s, half)
            pick(s - 1)
            for side, cols in halves.get(s, []):
                interleave(side, 0, cols)
            if s in quantise_after:
                quant_x(quantise_after[s], 0, whole)
        last_loads = held([P, 5, PICK], F32, "last_loads", "w1_first0")
        base_sb = last_loads[:, 0:4, :]
        fin_sb = last_loads[:, 4, :]
        nc.sync.dma_start(base_sb, base.rearrange("(m p) j -> p m j", p=P))
        nc.sync.dma_start(fin_sb, fin.partition_broadcast(P))
        pick(SLOTS - 1)
        interleave(1, 1, whole)
        interleave(0, 1, low, nc.vector.tensor_copy)
        interleave(0, 1, high, nc.vector.tensor_copy)
        quant_x(0, 1, low)
        quant_x(1, 1, whole)
        quant_x(0, 1, high)

        totals = []
        for m in range(PICK // P):
            bank = psum.tile([P, PICK], F32, name="score_bank", tag=bank_tag(2 + m // 2, m % 2))
            for b in range(2):
                nc.tensor.matmul_mx(
                    out=bank[:],
                    lhsT=x_codes[0, b][:, P * m : P * (m + 1)].bitcast(FP8X4),
                    lhsT_scale=x_scales[0, b][:, P * m : P * (m + 1)],
                    rhs=x_codes[1, b][:].bitcast(FP8X4),
                    rhs_scale=x_scales[1, b][:],
                    start=(b == 0),
                    stop=(b == 1),
                )
            totals.append(held([P, PICK], F32, "total%d" % m))
            nc.vector.tensor_tensor(totals[m][:], bank[:], base_sb[:, m, :], ALU.add)
        for m in range(PICK // P):
            result = held([P, PICK], F32, "result%d" % m)
            engine = nc.gpsimd if m == 0 else nc.vector
            engine.tensor_tensor(result[:], totals[m][:], fin_sb, ALU.mult)
            nc.sync.dma_start(out[P * m : P * (m + 1), :], result[:])
